import numpy as np
import ml_dtypes


def mxq(x, axis, fmt="e4m3"):
    dtype, down = {"e4m3": (ml_dtypes.float8_e4m3fn, 7), "e5m2": (ml_dtypes.float8_e5m2, 14)}[fmt]
    v = np.moveaxis(np.asarray(x, np.float32).astype(ml_dtypes.bfloat16).astype(np.float64), axis, -1)
    blocks = v.reshape(v.shape[:-1] + (-1, 32))
    amax = np.abs(blocks).max(-1, keepdims=True)
    byte = np.maximum(np.where(amax > 0, np.frexp(amax)[1] - 1 + 127, 0) - down, 1)
    scale = np.exp2(byte - 127.0)
    codes = (blocks / scale).astype(np.float32).astype(dtype).astype(np.float64)
    return np.moveaxis((codes * scale).reshape(v.shape), -1, axis)


WIDE = False


def mx_kscale(k):
    if not WIDE:
        return np.ones(k)
    levels = np.array([10, -10, 5, -5, 0])
    if k % 512:
        return np.exp2(np.random.permutation(np.resize(levels, k // 32))).repeat(32)
    a = np.empty((k // 512, 16))
    for p in range(k // 512):
        a[p, :8] = np.random.permutation(np.resize(levels, 8))
        for g in range(8):
            far = levels[np.abs(levels - a[p, g]) >= 10]
            a[p, g + 8] = far[np.random.randint(len(far))]
    return np.exp2(a.ravel()).repeat(32)


def f64(x):
    return np.asarray(x).astype(np.float64)


def striped8(idx):
    return np.asarray(idx).reshape(8, -1, 16).transpose(0, 2, 1).reshape(128, -1).astype(np.uint16)


def unstriped8(offs):
    return offs.reshape(8, 16, -1).transpose(0, 2, 1).reshape(8, -1).astype(np.int64)


def pick8(x, idx, run):
    r = np.arange(len(x))
    return x[r[:, None], idx[r % (8 * run) // run]]


E2M1 = np.array([0.0, 0.5, 1.0, 1.5, 2.0, 3.0, 4.0, 6.0, -0.0, -0.5, -1.0, -1.5, -2.0, -3.0, -4.0, -6.0])


def pack_weight(w, fmt):
    k, n = w.shape
    w = f64(np.asarray(w, np.float32).astype(ml_dtypes.bfloat16)).reshape(k // 32, 32, n)
    amax = np.abs(w).max(1)
    if fmt == "e4m3":
        byte = np.frexp(amax)[1] - 1 + 127 - 7
    else:
        mant, ex = np.frexp(amax / 6.0)
        byte = np.where(mant > 0.5, ex, ex - 1) + 127
    byte = np.clip(np.where(amax > 0, byte, 1), 1, 254)
    scaled = (w * np.exp2(127.0 - byte)[:, None, :]).reshape(k, n).astype(np.float32)
    by_word = np.ascontiguousarray(scaled.reshape(k // 512, 128, 4, n).transpose(0, 1, 3, 2))
    if fmt == "e4m3":
        words = by_word.astype(ml_dtypes.float8_e4m3fn).view(np.uint8)
    else:
        c = by_word.astype(ml_dtypes.float4_e2m1fn).view(np.uint8) & 0xF
        words = (c[..., 0::2] | (c[..., 1::2] << 4)).reshape(k // 512, 128, 2 * n)
    return np.ascontiguousarray(words), np.ascontiguousarray(byte.astype(np.uint8).reshape(k // 512, 16, n))


def unpack_weight(words, scales, fmt):
    g, _, n = scales.shape
    words = np.ascontiguousarray(words).reshape(g, 128, n, -1)
    if fmt == "e4m3":
        vals = words.view(ml_dtypes.float8_e4m3fn).astype(np.float64)
    else:
        nib = np.empty((g, 128, n, 4), np.uint8)
        nib[..., 0::2] = words & 0xF
        nib[..., 1::2] = words >> 4
        vals = E2M1[nib]
    vals = vals * np.repeat(np.exp2(scales.astype(np.float64) - 127.0), 8, axis=1)[..., None]
    return vals.transpose(0, 1, 3, 2).reshape(g * 512, n)


D, E, T, Q, I, G = 512, 512, 1024, 128, 512, 128


def setup_inputs():
    n = np.random.standard_normal
    idx = np.stack([np.random.permutation(T)[:I] for _ in range(8)])
    fd = mx_kscale(D)
    ft = mx_kscale(T)
    keysp = pack_weight(n((D, T)) / fd[:, None], "e2m1")
    return {
        "query": (n((D, Q)) * 0.5 / np.sqrt(D) * fd[:, None]).astype(np.float32),
        "keys_words": keysp[0],
        "keys_scales": keysp[1],
        "firm": (np.random.uniform(0.4, 1.0, (Q, 1))).astype(np.float32),
        "fac": (np.random.uniform(8.0, 32.0, (1, T)) * ft).astype(np.float32),
        "vals": (n((T, E)) / ft[:, None]).astype(np.float32),
        "offs": striped8(idx),
    }


def reference(query, keys_words, keys_scales, firm, fac, vals, offs):
    idx = unstriped8(offs)
    keysu = unpack_weight(keys_words, keys_scales, "e2m1")
    queryq = mxq(f64(query), 0, "e4m3")
    a = queryq.T @ keysu
    b = pick8(a, idx, 16).reshape(Q, G, I // G).max(axis=2)
    br = np.repeat(b, I // G, axis=1)
    dl = (br - pick8(a, idx, 16)) * f64(firm)
    df = np.zeros((Q, T))
    df[np.arange(Q)[:, None], idx[np.arange(Q) % 128 // 16]] = dl
    s = a + df
    p = np.exp(s - np.max(s, axis=1, keepdims=True))
    w = p * f64(fac) / np.sum(p, axis=1, keepdims=True)
    wt = w.T
    wtq = mxq(wt, 0, "e4m3")
    valsq = mxq(f64(vals), 0, "e4m3")
    o = wtq.T @ valsq
    return o

@@ -1,0 +1,195 @@
+from contextlib import ExitStack
+
+import concourse.mybir as mybir
+from concourse.masks import make_identity
+
+D, E, T, Q, SLOTS, GROUP = 512, 512, 1024, 128, 512, 4
+FLOPS = 2 * Q * T * D + 2 * Q * T * E
+
+F32 = mybir.dt.float32
+BF16 = mybir.dt.bfloat16
+I32 = mybir.dt.int32
+U32 = mybir.dt.uint32
+U16 = mybir.dt.uint16
+U8 = mybir.dt.uint8
+FP8X4 = mybir.dt.float8_e4m3fn_x4
+FP4X4 = mybir.dt.float4_e2m1fn_x4
+ALU = mybir.AluOpType
+ACT = mybir.ActivationFunctionType
+AXIS = mybir.AxisListType
+
+P = 128
+PACK = 4
+K_PASS = P * PACK
+PASSES = T // K_PASS
+SCORE_PIECES = ((0, 512), (512, 768), (768, 1024))
+HALF = SLOTS // 2
+OUT_HALF = E // 2
+
+
+def weave(ap_out, ap_in):
+    return (ap_out.rearrange("p (c i) t -> p c t i", i=4), ap_in.rearrange("p t (c i) -> p c t i", i=4))
+
+
+def tile_attend_levelled_heads_kernel(tc, query, keys_words, keys_scales, firm, fac, vals, offs, out):
+    nc = tc.nc
+    with ExitStack() as ctx:
+        lists = ctx.enter_context(tc.tile_pool(name="lists", bufs=1))
+        sb = ctx.enter_context(tc.tile_pool(name="sb", bufs=1))
+        ps = ctx.enter_context(tc.psum_pool(name="ps", bufs=1))
+
+        def tile(shape, dtype, name, tag=None):
+            return sb.tile(shape, dtype, name=name, tag=tag or name, align_bytes=64)
+
+        q_raw = tile([P, PACK, Q], F32, "q_raw", "raw1")
+        nc.sync.dma_start(out=q_raw[:], in_=query.rearrange("(p j) q -> p j q", j=PACK))
+        k_words = tile([P, 2 * T], U8, "k_words", "keys_fac")
+        nc.sync.dma_start(out=k_words[:].bitcast(I32), in_=keys_words[0].bitcast(I32))
+        offsets = lists.tile([P, SLOTS // 16], U16, name="offsets")
+        nc.sync.dma_start(offsets[:], offs)
+        v_raw0 = tile([P, PACK, E], F32, "v_raw0")
+        nc.sync.dma_start(out=v_raw0[:], in_=vals[0:K_PASS, :].rearrange("(p j) e -> p j e", j=PACK))
+
+        k_scales = tile([P, T], U8, "k_scales")
+        nc.vector.memset(k_scales[:].bitcast(I32), 0)
+        for quad in range(4):
+            nc.scalar.dma_start(
+                out=k_scales[32 * quad : 32 * quad + 4, :].bitcast(I32),
+                in_=keys_scales[0, 4 * quad : 4 * quad + 4, :].bitcast(I32),
+            )
+        firm_col = tile([P, 1], F32, "firm_col")
+        nc.gpsimd.dma_start(out=firm_col[:], in_=firm)
+
+        df = tile([P, T], F32, "df")
+        nc.gpsimd.memset(df[:], 0.0)
+        ident = tile([P, P], F32, "ident")
+        make_identity(nc, ident[:])
+
+        q_bf = tile([P, Q, PACK], BF16, "q_bf")
+        o, i = weave(q_bf[:], q_raw[:])
+        nc.vector.tensor_copy(out=o, in_=i)
+        q_codes = tile([P, Q], U32, "q_codes")
+        q_scales = tile([P, Q], U8, "q_scales")
+        nc.vector.quantize_mx(out=q_codes[:].bitcast(FP8X4), scales=q_scales[:], in_=q_bf[:].rearrange("p q j -> p (q j)"))
+
+        v_raw1 = tile([P, PACK, E], F32, "v_raw1", "raw1")
+        nc.sync.dma_start(out=v_raw1[:], in_=vals[K_PASS:T, :].rearrange("(p j) e -> p j e", j=PACK))
+
+        a = tile([P, T], F32, "a", "a_vbf0")
+        a_banks = []
+        for n, (c0, c1) in enumerate(SCORE_PIECES):
+            bank = ps.tile([P, c1 - c0], F32, name="a_bank%d" % n, tag="a_bank%d" % n)
+            a_banks.append(bank)
+            nc.tensor.matmul_mx(
+                out=bank[:],
+                lhsT=q_codes[:].bitcast(FP8X4),
+                lhsT_scale=q_scales[:],
+                rhs=k_words[:, 2 * c0 : 2 * c1].bitcast(FP4X4),
+                rhs_scale=k_scales[:, c0:c1],
+                start=True,
+                stop=True,
+            )
+            if n == 1:
+                nc.scalar.copy(out=a[:, c0:c1], in_=bank[:])
+            else:
+                nc.vector.tensor_copy(out=a[:, c0:c1], in_=bank[:])
+
+        fac_rows = tile([P, T], F32, "fac_rows", "keys_fac")
+        nc.sync.dma_start(out=fac_rows[:], in_=fac[0].partition_broadcast(P))
+
+        firm_rows = tile([P, SLOTS], F32, "firm_rows")
+        nc.vector.tensor_copy(out=firm_rows[:], in_=firm_col[:].to_broadcast([P, SLOTS]))
+
+        listed = tile([P, SLOTS], F32, "listed")
+        cols = HALF // 16
+        nc.vector.tensor_copy(out=listed[:, 0:HALF], in_=a[:].indirect(offsets[:, 0:cols]))
+        nc.scalar.activation(listed[:, HALF:SLOTS], a[:].indirect(offsets[:, cols : 2 * cols]), ACT.Copy)
+        best = tile([P, SLOTS // GROUP], F32, "best")
+        gap = tile([P, SLOTS], F32, "gap")
+        groups = HALF // GROUP
+        for h in range(2):
+            nc.vector.tensor_reduce(
+                out=best[:, h * groups : (h + 1) * groups],
+                in_=listed[:, h * HALF : (h + 1) * HALF].rearrange("p (g i) -> p g i", i=GROUP),
+                axis=AXIS.X,
+                op=ALU.max,
+            )
+        for h in range(2):
+            nc.vector.tensor_tensor(
+                out=gap[:, h * HALF : (h + 1) * HALF].rearrange("p (g i) -> p g i", i=GROUP),
+                in0=best[:, h * groups : (h + 1) * groups].unsqueeze(2).to_broadcast([P, groups, GROUP]),
+                in1=listed[:, h * HALF : (h + 1) * HALF].rearrange("p (g i) -> p g i", i=GROUP),
+                op=ALU.subtract,
+            )
+        nc.vector.tensor_tensor(out=df[:].indirect(offsets[:]), in0=gap[:], in1=firm_rows[:], op=ALU.mult)
+
+        v_bf = [tile([P, E, PACK], BF16, "v_bf0", "a_vbf0"), tile([P, E, PACK], BF16, "v_bf1")]
+        for g, raw in enumerate((v_raw0, v_raw1)):
+            o, i = weave(v_bf[g][:], raw[:])
+            nc.scalar.copy(out=o, in_=i)
+
+        s = tile([P, T], F32, "s", "s_vcodes")
+        for n, (c0, c1) in enumerate(SCORE_PIECES):
+            nc.vector.tensor_tensor(out=s[:, c0:c1], in0=a_banks[n][:], in1=df[:, c0:c1], op=ALU.add)
+        neg_s = tile([P, T], F32, "neg_s")
+        neg_max = tile([P, 1], F32, "neg_max")
+        nc.vector.tensor_scalar(
+            out=neg_s[:], in0=s[:], scalar1=-1.0, scalar2=None, op0=ALU.mult, op1=ALU.min, accum_out=neg_max[:]
+        )
+        p = tile([P, T], F32, "p", "raw1")
+        row_sum = tile([P, 1], F32, "row_sum")
+        nc.scalar.activation(out=p[:], in_=neg_s[:], func=ACT.Exp, bias=neg_max[:], scale=-1.0, accum_out=row_sum[:])
+
+        v_codes = tile([P, PASSES, E], U32, "v_codes", "s_vcodes")
+        v_scales = tile([P, PASSES, E], U8, "v_scales")
+        for g in range(PASSES):
+            nc.vector.quantize_mx(
+                out=v_codes[:, g, :].bitcast(FP8X4), scales=v_scales[:, g, :], in_=v_bf[g][:].rearrange("p e j -> p (e j)")
+            )
+
+        inv_sum = tile([P, 1], F32, "inv_sum")
+        nc.vector.reciprocal(out=inv_sum[:], in_=row_sum[:])
+
+        out_banks = [ps.tile([P, OUT_HALF], F32, name="out_bank%d" % h, tag="out_bank%d" % h) for h in range(2)]
+        w = [tile([P, K_PASS], BF16, "w%d" % g) for g in range(PASSES)]
+        for g in range(PASSES):
+            tok = slice(g * K_PASS, (g + 1) * K_PASS)
+            nc.vector.scalar_tensor_tensor(
+                out=w[g][:], in0=p[:, tok], scalar=inv_sum[:], in1=fac_rows[:, tok], op0=ALU.mult, op1=ALU.mult
+            )
+        wt_bf = []
+        for g in range(PASSES):
+            words = w[g][:].bitcast(F32)
+            turned = ps.tile([P, 2, Q], F32, name="turned%d" % g, tag="turned%d" % g)
+            for u in range(2):
+                nc.tensor.transpose(turned[:, u, :], words[:, u : K_PASS // 2 : 2], ident[:])
+            wt = tile([P, Q, PACK], BF16, "wt_bf%d" % g)
+            nc.scalar.copy(
+                out=wt[:].rearrange("p q j -> p (q j)").bitcast(F32).rearrange("p (q u) -> p q u", u=2),
+                in_=turned[:].rearrange("p u q -> p q u"),
+            )
+            wt_bf.append(wt)
+        for g in range(PASSES):
+            w_codes = tile([P, Q], U32, "w_codes%d" % g)
+            w_scales = tile([P, Q], U8, "w_scales%d" % g)
+            nc.vector.quantize_mx(
+                out=w_codes[:].bitcast(FP8X4), scales=w_scales[:], in_=wt_bf[g][:].rearrange("p q j -> p (q j)")
+            )
+            for h in range(2):
+                cols_e = slice(h * OUT_HALF, (h + 1) * OUT_HALF)
+                nc.tensor.matmul_mx(
+                    out=out_banks[h][:],
+                    lhsT=w_codes[:].bitcast(FP8X4),
+                    lhsT_scale=w_scales[:],
+                    rhs=v_codes[:, g, cols_e].bitcast(FP8X4),
+                    rhs_scale=v_scales[:, g, cols_e],
+                    start=(g == 0),
+                    stop=(g == PASSES - 1),
+                )
+
+        res0 = tile([P, OUT_HALF], F32, "res0")
+        nc.vector.tensor_copy(out=res0[:], in_=out_banks[0][:])
+        nc.sync.dma_start(out=out[:, 0:OUT_HALF], in_=res0[:])
+        res1 = tile([P, OUT_HALF], F32, "res1")
+        nc.scalar.copy(out=res1[:], in_=out_banks[1][:])
+        nc.scalar.dma_start(out=out[:, OUT_HALF:E], in_=res1[:])

@@ -22,7 +22,7 @@ P = 128
 PACK = 4
 K_PASS = P * PACK
 PASSES = T // K_PASS
-SCORE_PIECES = ((0, 512), (512, 768), (768, 1024))
+QUARTER = T // 4
 HALF = SLOTS // 2
 OUT_HALF = E // 2
 
@@ -41,27 +41,37 @@ def tile_attend_levelled_heads_kernel(tc, query, keys_words, keys_scales, firm, 
         def tile(shape, dtype, name, tag=None):
             return sb.tile(shape, dtype, name=name, tag=tag or name, align_bytes=64)
 
-        q_raw = tile([P, PACK, Q], F32, "q_raw", "raw1")
+        k_scales = tile([P, T], U8, "k_scales")
+        nc.vector.memset(k_scales[:].bitcast(I32), 0)
+        q_raw = tile([P, PACK, Q], F32, "q_raw", "raw1a")
         nc.sync.dma_start(out=q_raw[:], in_=query.rearrange("(p j) q -> p j q", j=PACK))
+        for quad in range(4):
+            nc.sync.dma_start(
+                out=k_scales[32 * quad : 32 * quad + 4, :].bitcast(I32),
+                in_=keys_scales[0, 4 * quad : 4 * quad + 4, :].bitcast(I32),
+            )
         k_words = tile([P, 2 * T], U8, "k_words", "keys_fac")
         nc.sync.dma_start(out=k_words[:].bitcast(I32), in_=keys_words[0].bitcast(I32))
         offsets = lists.tile([P, SLOTS // 16], U16, name="offsets")
         nc.sync.dma_start(offsets[:], offs)
-        v_raw0 = tile([P, PACK, E], F32, "v_raw0")
-        nc.sync.dma_start(out=v_raw0[:], in_=vals[0:K_PASS, :].rearrange("(p j) e -> p j e", j=PACK))
-
-        k_scales = tile([P, T], U8, "k_scales")
-        nc.vector.memset(k_scales[:].bitcast(I32), 0)
-        for quad in range(4):
-            nc.scalar.dma_start(
-                out=k_scales[32 * quad : 32 * quad + 4, :].bitcast(I32),
-                in_=keys_scales[0, 4 * quad : 4 * quad + 4, :].bitcast(I32),
-            )
+        vals0 = vals[0:K_PASS, :].rearrange("(p j) e -> p j e", j=PACK)
+        v_raw0a = tile([P, PACK, OUT_HALF], F32, "v_raw0a", "raw0a")
+        nc.sync.dma_start(out=v_raw0a[:], in_=vals0[:, :, 0:OUT_HALF])
+        v_raw0b = tile([P, PACK, OUT_HALF], F32, "v_raw0b")
+        nc.sync.dma_start(out=v_raw0b[:], in_=vals0[:, :, OUT_HALF:E])
+        one = tile([P, 1], F32, "one")
+        nc.gpsimd.memset(one[:], 1.0)
+        minus_one = tile([P, 1], F32, "minus_one")
+        nc.scalar.activation(out=minus_one[:], in_=one[:], func=ACT.Copy, scale=-1.0)
         firm_col = tile([P, 1], F32, "firm_col")
         nc.gpsimd.dma_start(out=firm_col[:], in_=firm)
+        neg_firm = tile([P, 1], F32, "neg_firm")
+        nc.gpsimd.tensor_scalar(out=neg_firm[:], in0=firm_col[:], scalar1=-1.0, scalar2=0.0, op0=ALU.mult, op1=ALU.add)
+        firm_less_one = tile([P, 1], F32, "firm_less_one")
+        nc.gpsimd.tensor_scalar(out=firm_less_one[:], in0=firm_col[:], scalar1=1.0, scalar2=-1.0, op0=ALU.mult, op1=ALU.add)
 
         df = tile([P, T], F32, "df")
-        nc.gpsimd.memset(df[:], 0.0)
+        nc.vector.memset(df[:], 0.0)
         ident = tile([P, P], F32, "ident")
         make_identity(nc, ident[:])
 
@@ -72,13 +82,22 @@ def tile_attend_levelled_heads_kernel(tc, query, keys_words, keys_scales, firm, 
         q_scales = tile([P, Q], U8, "q_scales")
         nc.vector.quantize_mx(out=q_codes[:].bitcast(FP8X4), scales=q_scales[:], in_=q_bf[:].rearrange("p q j -> p (q j)"))
 
-        v_raw1 = tile([P, PACK, E], F32, "v_raw1", "raw1")
-        nc.sync.dma_start(out=v_raw1[:], in_=vals[K_PASS:T, :].rearrange("(p j) e -> p j e", j=PACK))
+        vals1 = vals[K_PASS:T, :].rearrange("(p j) e -> p j e", j=PACK)
+        v_raw1a = tile([P, PACK, OUT_HALF], F32, "v_raw1a", "raw1a")
+        nc.sync.dma_start(out=v_raw1a[:], in_=vals1[:, :, 0:OUT_HALF])
+        v_raw1b = tile([P, PACK, OUT_HALF], F32, "v_raw1b")
+        nc.sync.dma_start(out=v_raw1b[:], in_=vals1[:, :, OUT_HALF:E])
+
+        v_bf0a = tile([P, OUT_HALF, PACK], BF16, "v_bf0a")
+        o, i = weave(v_bf0a[:], v_raw0a[:])
+        nc.scalar.copy(out=o, in_=i)
 
         a = tile([P, T], F32, "a", "a_vbf0")
+        a_max = [tile([P, 1], F32, "a_max%d" % g) for g in range(PASSES)]
         a_banks = []
-        for n, (c0, c1) in enumerate(SCORE_PIECES):
-            bank = ps.tile([P, c1 - c0], F32, name="a_bank%d" % n, tag="a_bank%d" % n)
+        for g in range(PASSES):
+            c0, c1 = g * K_PASS, (g + 1) * K_PASS
+            bank = ps.tile([P, K_PASS], F32, name="a_bank%d" % g, tag="a_bank%d" % g)
             a_banks.append(bank)
             nc.tensor.matmul_mx(
                 out=bank[:],
@@ -89,73 +108,104 @@ def tile_attend_levelled_heads_kernel(tc, query, keys_words, keys_scales, firm, 
                 start=True,
                 stop=True,
             )
-            if n == 1:
-                nc.scalar.copy(out=a[:, c0:c1], in_=bank[:])
-            else:
-                nc.vector.tensor_copy(out=a[:, c0:c1], in_=bank[:])
+            nc.vector.tensor_scalar(
+                out=a[:, c0:c1], in0=bank[:], scalar1=1.0, scalar2=None, op0=ALU.mult, op1=ALU.max, accum_out=a_max[g][:]
+            )
 
         fac_rows = tile([P, T], F32, "fac_rows", "keys_fac")
         nc.sync.dma_start(out=fac_rows[:], in_=fac[0].partition_broadcast(P))
 
-        firm_rows = tile([P, SLOTS], F32, "firm_rows")
-        nc.vector.tensor_copy(out=firm_rows[:], in_=firm_col[:].to_broadcast([P, SLOTS]))
-
-        listed = tile([P, SLOTS], F32, "listed")
+        neg_listed = tile([P, SLOTS], F32, "neg_listed", "raw0a")
         cols = HALF // 16
-        nc.vector.tensor_copy(out=listed[:, 0:HALF], in_=a[:].indirect(offsets[:, 0:cols]))
-        nc.scalar.activation(listed[:, HALF:SLOTS], a[:].indirect(offsets[:, cols : 2 * cols]), ACT.Copy)
-        best = tile([P, SLOTS // GROUP], F32, "best")
-        gap = tile([P, SLOTS], F32, "gap")
+        nc.vector.tensor_scalar(
+            out=neg_listed[:, 0:HALF], in0=a[:].indirect(offsets[:, 0:cols]), scalar1=-1.0, scalar2=0.0, op0=ALU.mult, op1=ALU.add
+        )
+        nc.scalar.activation(neg_listed[:, HALF:SLOTS], a[:].indirect(offsets[:, cols : 2 * cols]), ACT.Copy, scale=minus_one[:])
+        a_max_all = tile([P, 1], F32, "a_max_all")
+        nc.vector.tensor_tensor(out=a_max_all[:], in0=a_max[0][:], in1=a_max[1][:], op=ALU.max)
+        neg_best = tile([P, SLOTS // GROUP], F32, "neg_best")
+        pull = tile([P, SLOTS // GROUP], F32, "pull")
+        moved = tile([P, SLOTS], F32, "moved")
         groups = HALF // GROUP
+        halves = [slice(h * HALF, (h + 1) * HALF) for h in range(2)]
+        ghalves = [slice(h * groups, (h + 1) * groups) for h in range(2)]
         for h in range(2):
             nc.vector.tensor_reduce(
-                out=best[:, h * groups : (h + 1) * groups],
-                in_=listed[:, h * HALF : (h + 1) * HALF].rearrange("p (g i) -> p g i", i=GROUP),
+                out=neg_best[:, ghalves[h]],
+                in_=neg_listed[:, halves[h]].rearrange("p (g i) -> p g i", i=GROUP),
                 axis=AXIS.X,
-                op=ALU.max,
+                op=ALU.min,
             )
         for h in range(2):
-            nc.vector.tensor_tensor(
-                out=gap[:, h * HALF : (h + 1) * HALF].rearrange("p (g i) -> p g i", i=GROUP),
-                in0=best[:, h * groups : (h + 1) * groups].unsqueeze(2).to_broadcast([P, groups, GROUP]),
-                in1=listed[:, h * HALF : (h + 1) * HALF].rearrange("p (g i) -> p g i", i=GROUP),
-                op=ALU.subtract,
+            nc.vector.tensor_scalar(
+                out=pull[:, ghalves[h]], in0=neg_best[:, ghalves[h]], scalar1=neg_firm[:], scalar2=None, op0=ALU.mult
             )
-        nc.vector.tensor_tensor(out=df[:].indirect(offsets[:]), in0=gap[:], in1=firm_rows[:], op=ALU.mult)
-
-        v_bf = [tile([P, E, PACK], BF16, "v_bf0", "a_vbf0"), tile([P, E, PACK], BF16, "v_bf1")]
-        for g, raw in enumerate((v_raw0, v_raw1)):
-            o, i = weave(v_bf[g][:], raw[:])
-            nc.scalar.copy(out=o, in_=i)
-
-        s = tile([P, T], F32, "s", "s_vcodes")
-        for n, (c0, c1) in enumerate(SCORE_PIECES):
-            nc.vector.tensor_tensor(out=s[:, c0:c1], in0=a_banks[n][:], in1=df[:, c0:c1], op=ALU.add)
-        neg_s = tile([P, T], F32, "neg_s")
-        neg_max = tile([P, 1], F32, "neg_max")
+        for h in range(2):
+            nc.vector.scalar_tensor_tensor(
+                out=moved[:, halves[h]].rearrange("p (g i) -> p g i", i=GROUP),
+                in0=neg_listed[:, halves[h]].rearrange("p (g i) -> p g i", i=GROUP),
+                scalar=firm_less_one[:],
+                in1=pull[:, ghalves[h]].unsqueeze(2).to_broadcast([P, groups, GROUP]),
+                op0=ALU.mult,
+                op1=ALU.add,
+            )
+        moved2 = tile([P, SLOTS], F32, "moved2", "gap_vc")
+        row_max = tile([P, 1], F32, "row_max")
         nc.vector.tensor_scalar(
-            out=neg_s[:], in0=s[:], scalar1=-1.0, scalar2=None, op0=ALU.mult, op1=ALU.min, accum_out=neg_max[:]
+            out=moved2[:], in0=moved[:], scalar1=1.0, scalar2=a_max_all[:], op0=ALU.mult, op1=ALU.max, accum_out=row_max[:]
         )
-        p = tile([P, T], F32, "p", "raw1")
-        row_sum = tile([P, 1], F32, "row_sum")
-        nc.scalar.activation(out=p[:], in_=neg_s[:], func=ACT.Exp, bias=neg_max[:], scale=-1.0, accum_out=row_sum[:])
+        nc.vector.tensor_tensor(out=df[:].indirect(offsets[:]), in0=moved2[:], in1=neg_listed[:], op=ALU.add)
 
-        v_codes = tile([P, PASSES, E], U32, "v_codes", "s_vcodes")
-        v_scales = tile([P, PASSES, E], U8, "v_scales")
+        v_bf_mid = tile([P, E, PACK], BF16, "v_bf_mid", "a_vbf0")
+        o, i = weave(v_bf_mid[:, 0:OUT_HALF, :], v_raw0b[:])
+        nc.scalar.copy(out=o, in_=i)
+        o, i = weave(v_bf_mid[:, OUT_HALF:E, :], v_raw1a[:])
+        nc.scalar.copy(out=o, in_=i)
+
+        neg_max = tile([P, 1], F32, "neg_max")
+        nc.scalar.activation(out=neg_max[:], in_=row_max[:], func=ACT.Copy, scale=-1.0)
+        terms = tile([P, 4, K_PASS], F32, "terms")
+        sum_all = [tile([P, 1], F32, "sum_all%d" % g) for g in range(PASSES)]
+        sum_listed = tile([P, 1], F32, "sum_listed")
+        sum_moved = tile([P, 1], F32, "sum_moved")
         for g in range(PASSES):
-            nc.vector.quantize_mx(
-                out=v_codes[:, g, :].bitcast(FP8X4), scales=v_scales[:, g, :], in_=v_bf[g][:].rearrange("p e j -> p (e j)")
-            )
+            nc.scalar.activation(out=terms[:, g, :], in_=a_banks[g][:], func=ACT.Exp, bias=neg_max[:], accum_out=sum_all[g][:])
+        nc.scalar.activation(out=terms[:, 2, :], in_=neg_listed[:], func=ACT.Exp, bias=neg_max[:], scale=-1.0, accum_out=sum_listed[:])
+        sum_a = tile([P, 1], F32, "sum_a")
+        nc.scalar.activation(out=sum_a[:], in_=sum_all[0][:], func=ACT.Identity, bias=sum_all[1][:])
+        nc.scalar.activation(
+            out=terms[:, 3, :], in_=moved[:], func=ACT.Exp, bias=neg_max[:], accum_out=sum_moved[:]
+        )
+        sum_unlisted = tile([P, 1], F32, "sum_unlisted")
+        nc.scalar.activation(out=sum_unlisted[:], in_=sum_listed[:], func=ACT.Identity, bias=sum_a[:], scale=-1.0)
+        row_sum = tile([P, 1], F32, "row_sum", "rowsum_s_vbf")
+        nc.scalar.activation(out=row_sum[:], in_=sum_moved[:], func=ACT.Identity, bias=sum_unlisted[:])
 
+        p = [tile([P, K_PASS], F32, "p0", "raw1a"), tile([P, K_PASS], F32, "p1")]
         inv_sum = tile([P, 1], F32, "inv_sum")
-        nc.vector.reciprocal(out=inv_sum[:], in_=row_sum[:])
+        s_first = tile([P, QUARTER], F32, "s_first")
 
-        out_banks = [ps.tile([P, OUT_HALF], F32, name="out_bank%d" % h, tag="out_bank%d" % h) for h in range(2)]
+        def exp_quarter(n, s):
+            g, h = divmod(n, 2)
+            part = slice(h * QUARTER, (h + 1) * QUARTER)
+            nc.vector.tensor_tensor(out=s, in0=a_banks[g][:, part], in1=df[:, n * QUARTER : (n + 1) * QUARTER], op=ALU.add)
+            nc.scalar.activation(out=p[g][:, part], in_=s, func=ACT.Exp, bias=neg_max[:])
+
+        exp_quarter(0, s_first[:])
+        nc.vector.reciprocal(out=inv_sum[:], in_=row_sum[:])
+        s_rest = tile([P, 3 * QUARTER], F32, "s_rest", "rowsum_s_vbf")
+        for n in range(1, 4):
+            exp_quarter(n, s_rest[:, (n - 1) * QUARTER : n * QUARTER])
+
+        v_bf1b = tile([P, OUT_HALF, PACK], BF16, "v_bf1b", "rowsum_s_vbf")
+        o, i = weave(v_bf1b[:], v_raw1b[:])
+        nc.scalar.copy(out=o, in_=i)
+
         w = [tile([P, K_PASS], BF16, "w%d" % g) for g in range(PASSES)]
         for g in range(PASSES):
             tok = slice(g * K_PASS, (g + 1) * K_PASS)
             nc.vector.scalar_tensor_tensor(
-                out=w[g][:], in0=p[:, tok], scalar=inv_sum[:], in1=fac_rows[:, tok], op0=ALU.mult, op1=ALU.mult
+                out=w[g][:], in0=p[g][:], scalar=inv_sum[:], in1=fac_rows[:, tok], op0=ALU.mult, op1=ALU.mult
             )
         wt_bf = []
         for g in range(PASSES):
@@ -169,6 +219,21 @@ def tile_attend_levelled_heads_kernel(tc, query, keys_words, keys_scales, firm, 
                 in_=turned[:].rearrange("p u q -> p q u"),
             )
             wt_bf.append(wt)
+
+        v_parts = (v_bf0a[:], v_bf_mid[:, 0:OUT_HALF, :], v_bf_mid[:, OUT_HALF:E, :], v_bf1b[:])
+        vc_tags = ("gap_vc", "raw1a", "p1", "vc3")
+        v_codes, v_scales = [], []
+
+        def quantize_values(n):
+            codes = tile([P, OUT_HALF], U32, "v_codes%d" % n, vc_tags[n])
+            scales = tile([P, OUT_HALF], U8, "v_scales%d" % n)
+            nc.vector.quantize_mx(out=codes[:].bitcast(FP8X4), scales=scales[:], in_=v_parts[n].rearrange("p e j -> p (e j)"))
+            v_codes.append(codes)
+            v_scales.append(scales)
+
+        out_banks = [ps.tile([P, OUT_HALF], F32, name="out_bank%d" % h, tag="out_bank%d" % h) for h in range(2)]
+        for n in range(4):
+            quantize_values(n)
         for g in range(PASSES):
             w_codes = tile([P, Q], U32, "w_codes%d" % g)
             w_scales = tile([P, Q], U8, "w_scales%d" % g)
@@ -176,13 +241,12 @@ def tile_attend_levelled_heads_kernel(tc, query, keys_words, keys_scales, firm, 
                 out=w_codes[:].bitcast(FP8X4), scales=w_scales[:], in_=wt_bf[g][:].rearrange("p q j -> p (q j)")
             )
             for h in range(2):
-                cols_e = slice(h * OUT_HALF, (h + 1) * OUT_HALF)
                 nc.tensor.matmul_mx(
                     out=out_banks[h][:],
                     lhsT=w_codes[:].bitcast(FP8X4),
                     lhsT_scale=w_scales[:],
-                    rhs=v_codes[:, g, cols_e].bitcast(FP8X4),
-                    rhs_scale=v_scales[:, g, cols_e],
+                    rhs=v_codes[2 * g + h][:].bitcast(FP8X4),
+                    rhs_scale=v_scales[2 * g + h][:],
                     start=(g == 0),
                     stop=(g == PASSES - 1),
                 )

@@ -25,6 +25,8 @@ PASSES = T // K_PASS
 QUARTER = T // 4
 HALF = SLOTS // 2
 OUT_HALF = E // 2
+LATE = 128
+OUT_PIECES = ((0, 256), (256, 384), (384, 512))
 
 
 def weave(ap_out, ap_in):
@@ -41,6 +43,13 @@ def tile_attend_levelled_heads_kernel(tc, query, keys_words, keys_scales, firm, 
         def tile(shape, dtype, name, tag=None):
             return sb.tile(shape, dtype, name=name, tag=tag or name, align_bytes=64)
 
+        def weave_values(dst, raw):
+            o, i = weave(dst, raw)
+            nc.scalar.copy(out=o, in_=i)
+
+        def quantize(codes, scales, woven):
+            nc.vector.quantize_mx(out=codes.bitcast(FP8X4), scales=scales, in_=woven.rearrange("p c j -> p (c j)"))
+
         k_scales = tile([P, T], U8, "k_scales")
         nc.vector.memset(k_scales[:].bitcast(I32), 0)
         q_raw = tile([P, PACK, Q], F32, "q_raw", "raw1a")
@@ -52,13 +61,15 @@ def tile_attend_levelled_heads_kernel(tc, query, keys_words, keys_scales, firm, 
             )
         k_words = tile([P, 2 * T], U8, "k_words", "keys_fac")
         nc.sync.dma_start(out=k_words[:].bitcast(I32), in_=keys_words[0].bitcast(I32))
+        vals0 = vals[0:K_PASS, :].rearrange("(p j) e -> p j e", j=PACK)
+        v_raw0a = tile([P, PACK, LATE], F32, "v_raw0a")
+        nc.sync.dma_start(out=v_raw0a[:], in_=vals0[:, :, 256:384])
+        v_raw0c = tile([P, PACK, LATE], F32, "v_raw0c", "raw0a")
+        nc.sync.dma_start(out=v_raw0c[:], in_=vals0[:, :, 384:512])
         offsets = lists.tile([P, SLOTS // 16], U16, name="offsets")
         nc.sync.dma_start(offsets[:], offs)
-        vals0 = vals[0:K_PASS, :].rearrange("(p j) e -> p j e", j=PACK)
-        v_raw0a = tile([P, PACK, OUT_HALF], F32, "v_raw0a", "raw0a")
-        nc.sync.dma_start(out=v_raw0a[:], in_=vals0[:, :, 0:OUT_HALF])
         v_raw0b = tile([P, PACK, OUT_HALF], F32, "v_raw0b")
-        nc.sync.dma_start(out=v_raw0b[:], in_=vals0[:, :, OUT_HALF:E])
+        nc.sync.dma_start(out=v_raw0b[:], in_=vals0[:, :, 0:OUT_HALF])
         one = tile([P, 1], F32, "one")
         nc.gpsimd.memset(one[:], 1.0)
         minus_one = tile([P, 1], F32, "minus_one")
@@ -80,24 +91,24 @@ def tile_attend_levelled_heads_kernel(tc, query, keys_words, keys_scales, firm, 
         nc.vector.tensor_copy(out=o, in_=i)
         q_codes = tile([P, Q], U32, "q_codes")
         q_scales = tile([P, Q], U8, "q_scales")
-        nc.vector.quantize_mx(out=q_codes[:].bitcast(FP8X4), scales=q_scales[:], in_=q_bf[:].rearrange("p q j -> p (q j)"))
+        quantize(q_codes[:], q_scales[:], q_bf[:])
 
         vals1 = vals[K_PASS:T, :].rearrange("(p j) e -> p j e", j=PACK)
-        v_raw1a = tile([P, PACK, OUT_HALF], F32, "v_raw1a", "raw1a")
-        nc.sync.dma_start(out=v_raw1a[:], in_=vals1[:, :, 0:OUT_HALF])
-        v_raw1b = tile([P, PACK, OUT_HALF], F32, "v_raw1b")
-        nc.sync.dma_start(out=v_raw1b[:], in_=vals1[:, :, OUT_HALF:E])
+        v_raw1a = tile([P, PACK, E - LATE], F32, "v_raw1a", "raw1a")
+        nc.sync.dma_start(out=v_raw1a[:], in_=vals1[:, :, 0 : E - LATE])
+        v_raw1b = tile([P, PACK, LATE], F32, "v_raw1b")
+        nc.sync.dma_start(out=v_raw1b[:], in_=vals1[:, :, E - LATE : E])
 
         v_bf0a = tile([P, OUT_HALF, PACK], BF16, "v_bf0a")
-        o, i = weave(v_bf0a[:], v_raw0a[:])
-        nc.scalar.copy(out=o, in_=i)
+        weave_values(v_bf0a[:, 0:LATE, :], v_raw0a[:])
+        weave_values(v_bf0a[:, LATE:OUT_HALF, :], v_raw0c[:])
 
         a = tile([P, T], F32, "a", "a_vbf0")
-        a_max = [tile([P, 1], F32, "a_max%d" % g) for g in range(PASSES)]
+        a_part_max = tile([P, 4], F32, "a_part_max")
         a_banks = []
-        for g in range(PASSES):
-            c0, c1 = g * K_PASS, (g + 1) * K_PASS
-            bank = ps.tile([P, K_PASS], F32, name="a_bank%d" % g, tag="a_bank%d" % g)
+        for n in range(4):
+            c0, c1 = n * QUARTER, (n + 1) * QUARTER
+            bank = ps.tile([P, QUARTER], F32, name="a_bank%d" % n, tag="bank%d" % n)
             a_banks.append(bank)
             nc.tensor.matmul_mx(
                 out=bank[:],
@@ -109,7 +120,8 @@ def tile_attend_levelled_heads_kernel(tc, query, keys_words, keys_scales, firm, 
                 stop=True,
             )
             nc.vector.tensor_scalar(
-                out=a[:, c0:c1], in0=bank[:], scalar1=1.0, scalar2=None, op0=ALU.mult, op1=ALU.max, accum_out=a_max[g][:]
+                out=a[:, c0:c1], in0=bank[:], scalar1=1.0, scalar2=None, op0=ALU.mult, op1=ALU.max,
+                accum_out=a_part_max[:, n : n + 1],
             )
 
         fac_rows = tile([P, T], F32, "fac_rows", "keys_fac")
@@ -121,8 +133,8 @@ def tile_attend_levelled_heads_kernel(tc, query, keys_words, keys_scales, firm, 
             out=neg_listed[:, 0:HALF], in0=a[:].indirect(offsets[:, 0:cols]), scalar1=-1.0, scalar2=0.0, op0=ALU.mult, op1=ALU.add
         )
         nc.scalar.activation(neg_listed[:, HALF:SLOTS], a[:].indirect(offsets[:, cols : 2 * cols]), ACT.Copy, scale=minus_one[:])
-        a_max_all = tile([P, 1], F32, "a_max_all")
-        nc.vector.tensor_tensor(out=a_max_all[:], in0=a_max[0][:], in1=a_max[1][:], op=ALU.max)
+        a_max = tile([P, 1], F32, "a_max")
+        nc.vector.tensor_reduce(out=a_max[:], in_=a_part_max[:], axis=AXIS.X, op=ALU.max)
         neg_best = tile([P, SLOTS // GROUP], F32, "neg_best")
         pull = tile([P, SLOTS // GROUP], F32, "pull")
         moved = tile([P, SLOTS], F32, "moved")
@@ -149,68 +161,68 @@ def tile_attend_levelled_heads_kernel(tc, query, keys_words, keys_scales, firm, 
                 op0=ALU.mult,
                 op1=ALU.add,
             )
-        moved2 = tile([P, SLOTS], F32, "moved2", "gap_vc")
+        moved2 = tile([P, SLOTS], F32, "moved2")
         row_max = tile([P, 1], F32, "row_max")
         nc.vector.tensor_scalar(
-            out=moved2[:], in0=moved[:], scalar1=1.0, scalar2=a_max_all[:], op0=ALU.mult, op1=ALU.max, accum_out=row_max[:]
+            out=moved2[:], in0=moved[:], scalar1=1.0, scalar2=a_max[:], op0=ALU.mult, op1=ALU.max, accum_out=row_max[:]
         )
         nc.vector.tensor_tensor(out=df[:].indirect(offsets[:]), in0=moved2[:], in1=neg_listed[:], op=ALU.add)
 
-        v_bf_mid = tile([P, E, PACK], BF16, "v_bf_mid", "a_vbf0")
-        o, i = weave(v_bf_mid[:, 0:OUT_HALF, :], v_raw0b[:])
-        nc.scalar.copy(out=o, in_=i)
-        o, i = weave(v_bf_mid[:, OUT_HALF:E, :], v_raw1a[:])
-        nc.scalar.copy(out=o, in_=i)
+        v_codes0a = tile([P, OUT_HALF], U32, "v_codes0a")
+        v_scales0a = tile([P, OUT_HALF], U8, "v_scales0a")
+        for c0 in (0, LATE):
+            quantize(v_codes0a[:, c0 : c0 + LATE], v_scales0a[:, c0 : c0 + LATE], v_bf0a[:, c0 : c0 + LATE, :])
+
+        terms = tile([P, 2 * T], F32, "terms")
+        neg_a_max = tile([P, 1], F32, "neg_a_max", "minus_one")
+        nc.scalar.activation(out=neg_a_max[:], in_=a_max[:], func=ACT.Copy, scale=-1.0)
+        sum_all = tile([P, 1], F32, "sum_all")
+        sum_listed = tile([P, 1], F32, "sum_listed")
+        sum_moved = tile([P, 1], F32, "sum_moved")
+        nc.scalar.activation(out=terms[:, 0:T], in_=a[:], func=ACT.Exp, bias=neg_a_max[:], accum_out=sum_all[:])
+        nc.scalar.activation(
+            out=terms[:, T : T + SLOTS], in_=neg_listed[:], func=ACT.Exp, bias=neg_a_max[:], scale=-1.0, accum_out=sum_listed[:]
+        )
+        sum_unlisted = tile([P, 1], F32, "sum_unlisted", "unlisted_s_vbf")
+        nc.scalar.activation(out=sum_unlisted[:], in_=sum_listed[:], func=ACT.Identity, bias=sum_all[:], scale=-1.0)
 
         neg_max = tile([P, 1], F32, "neg_max")
         nc.scalar.activation(out=neg_max[:], in_=row_max[:], func=ACT.Copy, scale=-1.0)
-        terms = tile([P, 4, K_PASS], F32, "terms")
-        sum_all = [tile([P, 1], F32, "sum_all%d" % g) for g in range(PASSES)]
-        sum_listed = tile([P, 1], F32, "sum_listed")
-        sum_moved = tile([P, 1], F32, "sum_moved")
-        for g in range(PASSES):
-            nc.scalar.activation(out=terms[:, g, :], in_=a_banks[g][:], func=ACT.Exp, bias=neg_max[:], accum_out=sum_all[g][:])
-        nc.scalar.activation(out=terms[:, 2, :], in_=neg_listed[:], func=ACT.Exp, bias=neg_max[:], scale=-1.0, accum_out=sum_listed[:])
-        sum_a = tile([P, 1], F32, "sum_a")
-        nc.scalar.activation(out=sum_a[:], in_=sum_all[0][:], func=ACT.Identity, bias=sum_all[1][:])
-        nc.scalar.activation(
-            out=terms[:, 3, :], in_=moved[:], func=ACT.Exp, bias=neg_max[:], accum_out=sum_moved[:]
-        )
-        sum_unlisted = tile([P, 1], F32, "sum_unlisted")
-        nc.scalar.activation(out=sum_unlisted[:], in_=sum_listed[:], func=ACT.Identity, bias=sum_a[:], scale=-1.0)
-        row_sum = tile([P, 1], F32, "row_sum", "rowsum_s_vbf")
-        nc.scalar.activation(out=row_sum[:], in_=sum_moved[:], func=ACT.Identity, bias=sum_unlisted[:])
+        shift = tile([P, 1], F32, "shift")
+        nc.scalar.activation(out=shift[:], in_=row_max[:], func=ACT.Exp, bias=a_max[:], scale=-1.0)
+        nc.scalar.activation(out=terms[:, T + SLOTS : 2 * T], in_=moved[:], func=ACT.Exp, bias=neg_max[:], accum_out=sum_moved[:])
+        row_sum = tile([P, 1], F32, "row_sum")
+        nc.scalar.activation(out=row_sum[:], in_=sum_unlisted[:], func=ACT.Identity, bias=sum_moved[:], scale=shift[:])
 
-        p = [tile([P, K_PASS], F32, "p0", "raw1a"), tile([P, K_PASS], F32, "p1")]
+        v_bf_mid = tile([P, OUT_HALF + E - LATE, PACK], BF16, "v_bf_mid", "a_vbf0")
+        v_bf0b = v_bf_mid[:, 0:OUT_HALF, :]
+        v_bf1a = v_bf_mid[:, OUT_HALF : OUT_HALF + E - LATE, :]
+        for dst, raw, width in ((v_bf0b, v_raw0b, OUT_HALF), (v_bf1a, v_raw1a, E - LATE)):
+            for c0 in range(0, width, 128):
+                weave_values(dst[:, c0 : c0 + 128, :], raw[:, :, c0 : c0 + 128])
+
+        p = tile([P, T], F32, "p", "raw1a")
         inv_sum = tile([P, 1], F32, "inv_sum")
-        s_first = tile([P, QUARTER], F32, "s_first")
-
-        def exp_quarter(n, s):
-            g, h = divmod(n, 2)
-            part = slice(h * QUARTER, (h + 1) * QUARTER)
-            nc.vector.tensor_tensor(out=s, in0=a_banks[g][:, part], in1=df[:, n * QUARTER : (n + 1) * QUARTER], op=ALU.add)
-            nc.scalar.activation(out=p[g][:, part], in_=s, func=ACT.Exp, bias=neg_max[:])
-
-        exp_quarter(0, s_first[:])
         nc.vector.reciprocal(out=inv_sum[:], in_=row_sum[:])
-        s_rest = tile([P, 3 * QUARTER], F32, "s_rest", "rowsum_s_vbf")
-        for n in range(1, 4):
-            exp_quarter(n, s_rest[:, (n - 1) * QUARTER : n * QUARTER])
+        s = tile([P, T], F32, "s", "unlisted_s_vbf")
+        for n in range(4):
+            tok = slice(n * QUARTER, (n + 1) * QUARTER)
+            nc.vector.tensor_tensor(out=s[:, tok], in0=a_banks[n][:], in1=df[:, tok], op=ALU.add)
+            nc.scalar.activation(out=p[:, tok], in_=s[:, tok], func=ACT.Exp, bias=neg_max[:])
 
-        v_bf1b = tile([P, OUT_HALF, PACK], BF16, "v_bf1b", "rowsum_s_vbf")
-        o, i = weave(v_bf1b[:], v_raw1b[:])
-        nc.scalar.copy(out=o, in_=i)
+        v_bf1b = tile([P, LATE, PACK], BF16, "v_bf1b", "unlisted_s_vbf")
+        weave_values(v_bf1b[:], v_raw1b[:])
 
         w = [tile([P, K_PASS], BF16, "w%d" % g) for g in range(PASSES)]
         for g in range(PASSES):
             tok = slice(g * K_PASS, (g + 1) * K_PASS)
             nc.vector.scalar_tensor_tensor(
-                out=w[g][:], in0=p[g][:], scalar=inv_sum[:], in1=fac_rows[:, tok], op0=ALU.mult, op1=ALU.mult
+                out=w[g][:], in0=p[:, tok], scalar=inv_sum[:], in1=fac_rows[:, tok], op0=ALU.mult, op1=ALU.mult
             )
         wt_bf = []
         for g in range(PASSES):
             words = w[g][:].bitcast(F32)
-            turned = ps.tile([P, 2, Q], F32, name="turned%d" % g, tag="turned%d" % g)
+            turned = ps.tile([P, 2, Q], F32, name="turned%d" % g, tag="bank%d" % g)
             for u in range(2):
                 nc.tensor.transpose(turned[:, u, :], words[:, u : K_PASS // 2 : 2], ident[:])
             wt = tile([P, Q, PACK], BF16, "wt_bf%d" % g)
@@ -220,40 +232,45 @@ def tile_attend_levelled_heads_kernel(tc, query, keys_words, keys_scales, firm, 
             )
             wt_bf.append(wt)
 
-        v_parts = (v_bf0a[:], v_bf_mid[:, 0:OUT_HALF, :], v_bf_mid[:, OUT_HALF:E, :], v_bf1b[:])
-        vc_tags = ("gap_vc", "raw1a", "p1", "vc3")
-        v_codes, v_scales = [], []
+        w_codes = [tile([P, Q], U32, "w_codes%d" % g) for g in range(PASSES)]
+        w_scales = [tile([P, Q], U8, "w_scales%d" % g) for g in range(PASSES)]
+        v_codes_late = tile([P, OUT_HALF + E], U32, "v_codes_late", "raw1a")
+        v_scales_late = tile([P, OUT_HALF + E], U8, "v_scales_late")
+        v_codes0b, v_scales0b = v_codes_late[:, 0:OUT_HALF], v_scales_late[:, 0:OUT_HALF]
+        v_codes1, v_scales1 = v_codes_late[:, OUT_HALF:], v_scales_late[:, OUT_HALF:]
+        quantize(v_codes0b, v_scales0b, v_bf0b)
+        quantize(w_codes[0][:], w_scales[0][:], wt_bf[0][:])
+        for c0, c1 in OUT_PIECES[:2]:
+            quantize(v_codes1[:, c0:c1], v_scales1[:, c0:c1], v_bf1a[:, c0:c1, :])
+        quantize(v_codes1[:, E - LATE : E], v_scales1[:, E - LATE : E], v_bf1b[:])
+        quantize(w_codes[1][:], w_scales[1][:], wt_bf[1][:])
 
-        def quantize_values(n):
-            codes = tile([P, OUT_HALF], U32, "v_codes%d" % n, vc_tags[n])
-            scales = tile([P, OUT_HALF], U8, "v_scales%d" % n)
-            nc.vector.quantize_mx(out=codes[:].bitcast(FP8X4), scales=scales[:], in_=v_parts[n].rearrange("p e j -> p (e j)"))
-            v_codes.append(codes)
-            v_scales.append(scales)
-
-        out_banks = [ps.tile([P, OUT_HALF], F32, name="out_bank%d" % h, tag="out_bank%d" % h) for h in range(2)]
-        for n in range(4):
-            quantize_values(n)
-        for g in range(PASSES):
-            w_codes = tile([P, Q], U32, "w_codes%d" % g)
-            w_scales = tile([P, Q], U8, "w_scales%d" % g)
-            nc.vector.quantize_mx(
-                out=w_codes[:].bitcast(FP8X4), scales=w_scales[:], in_=wt_bf[g][:].rearrange("p q j -> p (q j)")
-            )
-            for h in range(2):
+        rhs0 = [
+            (v_codes0b, v_scales0b),
+            (v_codes0a[:, 0:LATE], v_scales0a[:, 0:LATE]),
+            (v_codes0a[:, LATE:OUT_HALF], v_scales0a[:, LATE:OUT_HALF]),
+        ]
+        rhs1 = [(v_codes1[:, c0:c1], v_scales1[:, c0:c1]) for c0, c1 in OUT_PIECES]
+        out_banks = [
+            ps.tile([P, c1 - c0], F32, name="out_bank%d" % h, tag="out_bank%d" % h) for h, (c0, c1) in enumerate(OUT_PIECES)
+        ]
+        for g, rhs in enumerate((rhs0, rhs1)):
+            for h in range(3):
                 nc.tensor.matmul_mx(
                     out=out_banks[h][:],
-                    lhsT=w_codes[:].bitcast(FP8X4),
-                    lhsT_scale=w_scales[:],
-                    rhs=v_codes[2 * g + h][:].bitcast(FP8X4),
-                    rhs_scale=v_scales[2 * g + h][:],
+                    lhsT=w_codes[g][:].bitcast(FP8X4),
+                    lhsT_scale=w_scales[g][:],
+                    rhs=rhs[h][0].bitcast(FP8X4),
+                    rhs_scale=rhs[h][1],
                     start=(g == 0),
                     stop=(g == PASSES - 1),
                 )
 
-        res0 = tile([P, OUT_HALF], F32, "res0")
-        nc.vector.tensor_copy(out=res0[:], in_=out_banks[0][:])
-        nc.sync.dma_start(out=out[:, 0:OUT_HALF], in_=res0[:])
-        res1 = tile([P, OUT_HALF], F32, "res1")
-        nc.scalar.copy(out=res1[:], in_=out_banks[1][:])
-        nc.scalar.dma_start(out=out[:, OUT_HALF:E], in_=res1[:])
+        for h, (c0, c1) in enumerate(OUT_PIECES):
+            res = tile([P, c1 - c0], F32, "res%d" % h)
+            if h == 1:
+                nc.scalar.copy(out=res[:], in_=out_banks[h][:])
+                nc.scalar.dma_start(out=out[:, c0:c1], in_=res[:])
+            else:
+                nc.vector.tensor_copy(out=res[:], in_=out_banks[h][:])
+                nc.sync.dma_start(out=out[:, c0:c1], in_=res[:])

from contextlib import ExitStack

import concourse.mybir as mybir
from concourse.masks import make_identity

D, E, T, Q, SLOTS, GROUP = 512, 512, 1024, 128, 512, 4
FLOPS = 2 * Q * T * D + 2 * Q * T * E

F32 = mybir.dt.float32
BF16 = mybir.dt.bfloat16
I32 = mybir.dt.int32
U32 = mybir.dt.uint32
U16 = mybir.dt.uint16
U8 = mybir.dt.uint8
FP8X4 = mybir.dt.float8_e4m3fn_x4
FP4X4 = mybir.dt.float4_e2m1fn_x4
ALU = mybir.AluOpType
ACT = mybir.ActivationFunctionType
AXIS = mybir.AxisListType

P = 128
PACK = 4
K_PASS = P * PACK
PASSES = T // K_PASS
QUARTER = T // 4
HALF = SLOTS // 2
OUT_HALF = E // 2
LATE = 128
OUT_PIECES = ((0, 256), (256, 384), (384, 512))


def weave(ap_out, ap_in):
    return (ap_out.rearrange("p (c i) t -> p c t i", i=4), ap_in.rearrange("p t (c i) -> p c t i", i=4))


def tile_attend_levelled_heads_kernel(tc, query, keys_words, keys_scales, firm, fac, vals, offs, out):
    nc = tc.nc
    with ExitStack() as ctx:
        lists = ctx.enter_context(tc.tile_pool(name="lists", bufs=1))
        sb = ctx.enter_context(tc.tile_pool(name="sb", bufs=1))
        ps = ctx.enter_context(tc.psum_pool(name="ps", bufs=1))

        def tile(shape, dtype, name, tag=None):
            return sb.tile(shape, dtype, name=name, tag=tag or name, align_bytes=64)

        def weave_values(dst, raw):
            o, i = weave(dst, raw)
            nc.scalar.copy(out=o, in_=i)

        def quantize(codes, scales, woven):
            nc.vector.quantize_mx(out=codes.bitcast(FP8X4), scales=scales, in_=woven.rearrange("p c j -> p (c j)"))

        k_scales = tile([P, T], U8, "k_scales")
        nc.vector.memset(k_scales[:].bitcast(I32), 0)
        q_raw = tile([P, PACK, Q], F32, "q_raw", "raw1a")
        nc.sync.dma_start(out=q_raw[:], in_=query.rearrange("(p j) q -> p j q", j=PACK))
        for quad in range(4):
            nc.sync.dma_start(
                out=k_scales[32 * quad : 32 * quad + 4, :].bitcast(I32),
                in_=keys_scales[0, 4 * quad : 4 * quad + 4, :].bitcast(I32),
            )
        k_words = tile([P, 2 * T], U8, "k_words", "keys_fac")
        nc.sync.dma_start(out=k_words[:].bitcast(I32), in_=keys_words[0].bitcast(I32))
        vals0 = vals[0:K_PASS, :].rearrange("(p j) e -> p j e", j=PACK)
        v_raw0a = tile([P, PACK, LATE], F32, "v_raw0a")
        nc.sync.dma_start(out=v_raw0a[:], in_=vals0[:, :, 256:384])
        v_raw0c = tile([P, PACK, LATE], F32, "v_raw0c", "raw0a")
        nc.sync.dma_start(out=v_raw0c[:], in_=vals0[:, :, 384:512])
        offsets = lists.tile([P, SLOTS // 16], U16, name="offsets")
        nc.sync.dma_start(offsets[:], offs)
        v_raw0b = tile([P, PACK, OUT_HALF], F32, "v_raw0b")
        nc.sync.dma_start(out=v_raw0b[:], in_=vals0[:, :, 0:OUT_HALF])
        one = tile([P, 1], F32, "one")
        nc.gpsimd.memset(one[:], 1.0)
        minus_one = tile([P, 1], F32, "minus_one")
        nc.scalar.activation(out=minus_one[:], in_=one[:], func=ACT.Copy, scale=-1.0)
        firm_col = tile([P, 1], F32, "firm_col")
        nc.gpsimd.dma_start(out=firm_col[:], in_=firm)
        neg_firm = tile([P, 1], F32, "neg_firm")
        nc.gpsimd.tensor_scalar(out=neg_firm[:], in0=firm_col[:], scalar1=-1.0, scalar2=0.0, op0=ALU.mult, op1=ALU.add)
        firm_less_one = tile([P, 1], F32, "firm_less_one")
        nc.gpsimd.tensor_scalar(out=firm_less_one[:], in0=firm_col[:], scalar1=1.0, scalar2=-1.0, op0=ALU.mult, op1=ALU.add)

        df = tile([P, T], F32, "df")
        nc.vector.memset(df[:], 0.0)
        ident = tile([P, P], F32, "ident")
        make_identity(nc, ident[:])

        q_bf = tile([P, Q, PACK], BF16, "q_bf")
        o, i = weave(q_bf[:], q_raw[:])
        nc.vector.tensor_copy(out=o, in_=i)
        q_codes = tile([P, Q], U32, "q_codes")
        q_scales = tile([P, Q], U8, "q_scales")
        quantize(q_codes[:], q_scales[:], q_bf[:])

        vals1 = vals[K_PASS:T, :].rearrange("(p j) e -> p j e", j=PACK)
        v_raw1a = tile([P, PACK, E - LATE], F32, "v_raw1a", "raw1a")
        nc.sync.dma_start(out=v_raw1a[:], in_=vals1[:, :, 0 : E - LATE])
        v_raw1b = tile([P, PACK, LATE], F32, "v_raw1b")
        nc.sync.dma_start(out=v_raw1b[:], in_=vals1[:, :, E - LATE : E])

        v_bf0a = tile([P, OUT_HALF, PACK], BF16, "v_bf0a")
        weave_values(v_bf0a[:, 0:LATE, :], v_raw0a[:])
        weave_values(v_bf0a[:, LATE:OUT_HALF, :], v_raw0c[:])

        a = tile([P, T], F32, "a", "a_vbf0")
        a_part_max = tile([P, 4], F32, "a_part_max")
        a_banks = []
        for n in range(4):
            c0, c1 = n * QUARTER, (n + 1) * QUARTER
            bank = ps.tile([P, QUARTER], F32, name="a_bank%d" % n, tag="bank%d" % n)
            a_banks.append(bank)
            nc.tensor.matmul_mx(
                out=bank[:],
                lhsT=q_codes[:].bitcast(FP8X4),
                lhsT_scale=q_scales[:],
                rhs=k_words[:, 2 * c0 : 2 * c1].bitcast(FP4X4),
                rhs_scale=k_scales[:, c0:c1],
                start=True,
                stop=True,
            )
            nc.vector.tensor_scalar(
                out=a[:, c0:c1], in0=bank[:], scalar1=1.0, scalar2=None, op0=ALU.mult, op1=ALU.max,
                accum_out=a_part_max[:, n : n + 1],
            )

        fac_rows = tile([P, T], F32, "fac_rows", "keys_fac")
        nc.sync.dma_start(out=fac_rows[:], in_=fac[0].partition_broadcast(P))

        neg_listed = tile([P, SLOTS], F32, "neg_listed", "raw0a")
        cols = HALF // 16
        nc.vector.tensor_scalar(
            out=neg_listed[:, 0:HALF], in0=a[:].indirect(offsets[:, 0:cols]), scalar1=-1.0, scalar2=0.0, op0=ALU.mult, op1=ALU.add
        )
        nc.scalar.activation(neg_listed[:, HALF:SLOTS], a[:].indirect(offsets[:, cols : 2 * cols]), ACT.Copy, scale=minus_one[:])
        a_max = tile([P, 1], F32, "a_max")
        nc.vector.tensor_reduce(out=a_max[:], in_=a_part_max[:], axis=AXIS.X, op=ALU.max)
        neg_best = tile([P, SLOTS // GROUP], F32, "neg_best")
        pull = tile([P, SLOTS // GROUP], F32, "pull")
        moved = tile([P, SLOTS], F32, "moved")
        groups = HALF // GROUP
        halves = [slice(h * HALF, (h + 1) * HALF) for h in range(2)]
        ghalves = [slice(h * groups, (h + 1) * groups) for h in range(2)]
        for h in range(2):
            nc.vector.tensor_reduce(
                out=neg_best[:, ghalves[h]],
                in_=neg_listed[:, halves[h]].rearrange("p (g i) -> p g i", i=GROUP),
                axis=AXIS.X,
                op=ALU.min,
            )
        for h in range(2):
            nc.vector.tensor_scalar(
                out=pull[:, ghalves[h]], in0=neg_best[:, ghalves[h]], scalar1=neg_firm[:], scalar2=None, op0=ALU.mult
            )
        for h in range(2):
            nc.vector.scalar_tensor_tensor(
                out=moved[:, halves[h]].rearrange("p (g i) -> p g i", i=GROUP),
                in0=neg_listed[:, halves[h]].rearrange("p (g i) -> p g i", i=GROUP),
                scalar=firm_less_one[:],
                in1=pull[:, ghalves[h]].unsqueeze(2).to_broadcast([P, groups, GROUP]),
                op0=ALU.mult,
                op1=ALU.add,
            )
        moved2 = tile([P, SLOTS], F32, "moved2")
        row_max = tile([P, 1], F32, "row_max")
        nc.vector.tensor_scalar(
            out=moved2[:], in0=moved[:], scalar1=1.0, scalar2=a_max[:], op0=ALU.mult, op1=ALU.max, accum_out=row_max[:]
        )
        nc.vector.tensor_tensor(out=df[:].indirect(offsets[:]), in0=moved2[:], in1=neg_listed[:], op=ALU.add)

        v_codes0a = tile([P, OUT_HALF], U32, "v_codes0a")
        v_scales0a = tile([P, OUT_HALF], U8, "v_scales0a")
        for c0 in (0, LATE):
            quantize(v_codes0a[:, c0 : c0 + LATE], v_scales0a[:, c0 : c0 + LATE], v_bf0a[:, c0 : c0 + LATE, :])

        terms = tile([P, 2 * T], F32, "terms")
        neg_a_max = tile([P, 1], F32, "neg_a_max", "minus_one")
        nc.scalar.activation(out=neg_a_max[:], in_=a_max[:], func=ACT.Copy, scale=-1.0)
        sum_all = tile([P, 1], F32, "sum_all")
        sum_listed = tile([P, 1], F32, "sum_listed")
        sum_moved = tile([P, 1], F32, "sum_moved")
        nc.scalar.activation(out=terms[:, 0:T], in_=a[:], func=ACT.Exp, bias=neg_a_max[:], accum_out=sum_all[:])
        nc.scalar.activation(
            out=terms[:, T : T + SLOTS], in_=neg_listed[:], func=ACT.Exp, bias=neg_a_max[:], scale=-1.0, accum_out=sum_listed[:]
        )
        sum_unlisted = tile([P, 1], F32, "sum_unlisted", "unlisted_s_vbf")
        nc.scalar.activation(out=sum_unlisted[:], in_=sum_listed[:], func=ACT.Identity, bias=sum_all[:], scale=-1.0)

        neg_max = tile([P, 1], F32, "neg_max")
        nc.scalar.activation(out=neg_max[:], in_=row_max[:], func=ACT.Copy, scale=-1.0)
        shift = tile([P, 1], F32, "shift")
        nc.scalar.activation(out=shift[:], in_=row_max[:], func=ACT.Exp, bias=a_max[:], scale=-1.0)
        nc.scalar.activation(out=terms[:, T + SLOTS : 2 * T], in_=moved[:], func=ACT.Exp, bias=neg_max[:], accum_out=sum_moved[:])
        row_sum = tile([P, 1], F32, "row_sum")
        nc.scalar.activation(out=row_sum[:], in_=sum_unlisted[:], func=ACT.Identity, bias=sum_moved[:], scale=shift[:])

        v_bf_mid = tile([P, OUT_HALF + E - LATE, PACK], BF16, "v_bf_mid", "a_vbf0")
        v_bf0b = v_bf_mid[:, 0:OUT_HALF, :]
        v_bf1a = v_bf_mid[:, OUT_HALF : OUT_HALF + E - LATE, :]
        for dst, raw, width in ((v_bf0b, v_raw0b, OUT_HALF), (v_bf1a, v_raw1a, E - LATE)):
            for c0 in range(0, width, 128):
                weave_values(dst[:, c0 : c0 + 128, :], raw[:, :, c0 : c0 + 128])

        p = tile([P, T], F32, "p", "raw1a")
        inv_sum = tile([P, 1], F32, "inv_sum")
        nc.vector.reciprocal(out=inv_sum[:], in_=row_sum[:])
        s = tile([P, T], F32, "s", "unlisted_s_vbf")
        for n in range(4):
            tok = slice(n * QUARTER, (n + 1) * QUARTER)
            nc.vector.tensor_tensor(out=s[:, tok], in0=a_banks[n][:], in1=df[:, tok], op=ALU.add)
            nc.scalar.activation(out=p[:, tok], in_=s[:, tok], func=ACT.Exp, bias=neg_max[:])

        v_bf1b = tile([P, LATE, PACK], BF16, "v_bf1b", "unlisted_s_vbf")
        weave_values(v_bf1b[:], v_raw1b[:])

        w = [tile([P, K_PASS], BF16, "w%d" % g) for g in range(PASSES)]
        for g in range(PASSES):
            tok = slice(g * K_PASS, (g + 1) * K_PASS)
            nc.vector.scalar_tensor_tensor(
                out=w[g][:], in0=p[:, tok], scalar=inv_sum[:], in1=fac_rows[:, tok], op0=ALU.mult, op1=ALU.mult
            )
        wt_bf = []
        for g in range(PASSES):
            words = w[g][:].bitcast(F32)
            turned = ps.tile([P, 2, Q], F32, name="turned%d" % g, tag="bank%d" % g)
            for u in range(2):
                nc.tensor.transpose(turned[:, u, :], words[:, u : K_PASS // 2 : 2], ident[:])
            wt = tile([P, Q, PACK], BF16, "wt_bf%d" % g)
            nc.scalar.copy(
                out=wt[:].rearrange("p q j -> p (q j)").bitcast(F32).rearrange("p (q u) -> p q u", u=2),
                in_=turned[:].rearrange("p u q -> p q u"),
            )
            wt_bf.append(wt)

        w_codes = [tile([P, Q], U32, "w_codes%d" % g) for g in range(PASSES)]
        w_scales = [tile([P, Q], U8, "w_scales%d" % g) for g in range(PASSES)]
        v_codes_late = tile([P, OUT_HALF + E], U32, "v_codes_late", "raw1a")
        v_scales_late = tile([P, OUT_HALF + E], U8, "v_scales_late")
        v_codes0b, v_scales0b = v_codes_late[:, 0:OUT_HALF], v_scales_late[:, 0:OUT_HALF]
        v_codes1, v_scales1 = v_codes_late[:, OUT_HALF:], v_scales_late[:, OUT_HALF:]
        quantize(v_codes0b, v_scales0b, v_bf0b)
        quantize(w_codes[0][:], w_scales[0][:], wt_bf[0][:])
        for c0, c1 in OUT_PIECES[:2]:
            quantize(v_codes1[:, c0:c1], v_scales1[:, c0:c1], v_bf1a[:, c0:c1, :])
        quantize(v_codes1[:, E - LATE : E], v_scales1[:, E - LATE : E], v_bf1b[:])
        quantize(w_codes[1][:], w_scales[1][:], wt_bf[1][:])

        rhs0 = [
            (v_codes0b, v_scales0b),
            (v_codes0a[:, 0:LATE], v_scales0a[:, 0:LATE]),
            (v_codes0a[:, LATE:OUT_HALF], v_scales0a[:, LATE:OUT_HALF]),
        ]
        rhs1 = [(v_codes1[:, c0:c1], v_scales1[:, c0:c1]) for c0, c1 in OUT_PIECES]
        out_banks = [
            ps.tile([P, c1 - c0], F32, name="out_bank%d" % h, tag="out_bank%d" % h) for h, (c0, c1) in enumerate(OUT_PIECES)
        ]
        for g, rhs in enumerate((rhs0, rhs1)):
            for h in range(3):
                nc.tensor.matmul_mx(
                    out=out_banks[h][:],
                    lhsT=w_codes[g][:].bitcast(FP8X4),
                    lhsT_scale=w_scales[g][:],
                    rhs=rhs[h][0].bitcast(FP8X4),
                    rhs_scale=rhs[h][1],
                    start=(g == 0),
                    stop=(g == PASSES - 1),
                )

        for h, (c0, c1) in enumerate(OUT_PIECES):
            res = tile([P, c1 - c0], F32, "res%d" % h)
            if h == 1:
                nc.scalar.copy(out=res[:], in_=out_banks[h][:])
                nc.scalar.dma_start(out=out[:, c0:c1], in_=res[:])
            else:
                nc.vector.tensor_copy(out=res[:], in_=out_banks[h][:])
                nc.sync.dma_start(out=out[:, c0:c1], in_=res[:])
